import numpy as np, ml_dtypes
CORES = [12,28,44,60,3,19,35,51]
N = 8
C = 512
SIGN = [[1,1,1,1,1,1,1,1],[1,-1,1,-1,1,-1,1,-1],[1,1,-1,-1,1,1,-1,-1],[1,-1,-1,1,1,-1,-1,1],[1,1,1,1,-1,-1,-1,-1],[1,-1,1,-1,-1,1,-1,1],[1,1,-1,-1,-1,-1,1,1],[1,-1,-1,1,-1,1,1,-1]]
def setup_inputs(rng):
    return {"x": rng.standard_normal((N, 128, C), dtype=np.float32).astype(ml_dtypes.bfloat16), "w": (rng.standard_normal((N, 128, 128), dtype=np.float32) / 11).astype(ml_dtypes.bfloat16)}
def setup_inputs_big(rng):
    d = setup_inputs(rng)
    for k in ("x", "w"): d[k] = (d[k].astype(np.float32) * 1024.0).astype(d[k].dtype)
    return d
def setup_inputs_small(rng):
    d = setup_inputs(rng)
    for k in ("x", "w"): d[k] = (d[k].astype(np.float32) * (1 / 1024.0)).astype(d[k].dtype)
    return d
def setup_inputs_apart(rng):
    d = setup_inputs(rng)
    f = (10.0 ** rng.permutation(np.linspace(-1.5, 1.5, N))).astype(np.float32).reshape(N, 1, 1)
    for k in ("x", "w"): d[k] = (d[k].astype(np.float32) * f).astype(d[k].dtype)
    return d
def reference(x, w):
    X = x.astype(np.float64)
    y = np.stack([w[r].astype(np.float64).T @ sum(SIGN[r][j] * X[j] for j in range(N)) for r in range(N)])
    return {"y": y.astype(ml_dtypes.bfloat16)}

@@ -1,0 +1,151 @@
+from concourse.bass import DstId, RemoteDMATransfer
+from concourse.mybir import AluOpType
+
+N = 8
+C = 512
+K = 128
+
+SCRATCH = {
+    "dx": ("dram", [128, C], "bfloat16"),
+    "xin": ("sbuf", [128, N * C], "bfloat16"),
+    "ws": ("sbuf", [128, K], "bfloat16"),
+    "m1": ("sbuf", [128, K], "bfloat16"),
+    "nw": ("sbuf", [128, K], "bfloat16"),
+    "ys": ("sbuf", [128, C], "bfloat16"),
+    "acc": ("psum", [128, C], "float32"),
+}
+SEMAPHORES = ["ldx", "ldo", "ldw", "fill", "neg", "mm", "cp", "st", "relay", "sent"] + ["a%d" % j for j in range(N)]
+
+HELPERS = 2
+CAP_HELPER = 2
+CAP_RANK = 3
+
+
+def _engines(mask):
+    return [1 << b for b in range(mask.bit_length()) if (mask >> b) & 1]
+
+
+def _join(bits):
+    m = 0
+    for b in bits:
+        m |= b
+    return m
+
+
+def _plan(T, topo):
+    cores = list(T.cores)
+    half = len(cores) // 2
+    out = []
+    for j, me in enumerate(cores):
+        ch = topo.chip(me)
+
+        def rot(d):
+            return (cores.index(d) - j) % half
+
+        plane = sorted([d for d in cores if topo.same_plane(ch, topo.chip(d))], key=rot)
+        cross = sorted([d for d in cores if d != me and d not in plane], key=rot)
+        cand = [c for c in range(topo.CHIPS * topo.CORES_PER_CHIP)
+                if topo.chip(c) == ch and c not in cores and topo.die(c) == topo.die(me)]
+        cand.sort(key=lambda c: not all(topo.may_write(c, d) for d in cross))
+        helpers = cand[:HELPERS]
+        senders = helpers + [me]
+        caps = [CAP_HELPER] * len(helpers) + [CAP_RANK]
+        jobs = {s: [] for s in senders}
+        for d in cross + plane:
+            for s, cap in zip(senders, caps):
+                if len(jobs[s]) < cap and topo.may_write(s, d):
+                    jobs[s].append(d)
+                    break
+        out.append((helpers, jobs))
+    return out
+
+
+def _send(g, T, topo, core, j, dests):
+    n = 0
+    for d in dests:
+        rid, pid, _ = topo.addr(d)
+        m = topo.mask(core, d)
+        g.remote_dma(out_ap=T.xin[:, j * C:(j + 1) * C], in_ap=T.dx[:], remote_sem=T.sem["a%d" % j],
+                     local_sem=T.sem.sent, pid=pid, routing_id=rid, dma_engine_mask=m)
+        n += len(_engines(m))
+    return n
+
+
+def rank_program(g, core, T, topo):
+    S = T.sem
+    plan = _plan(T, topo)
+    cores = list(T.cores)
+    rank = T.rank_of(core)
+
+    if rank is None:
+        for j, (helpers, jobs) in enumerate(plan):
+            if core in helpers:
+                on = topo.mask(cores[j], core)
+                off = topo.mask(cores[j], jobs[cores[j]][0])
+                share = len(_engines(on & ~off)) // len(helpers)
+                g.wait_ge(S.relay, share)
+                n = _send(g, T, topo, core, j, jobs[core])
+                g.wait_ge(S.sent, n)
+        return
+
+    helpers, jobs = plan[rank]
+    sign = T.tables["SIGN"][rank]
+    own = T.xin[:, rank * C:(rank + 1) * C]
+
+    g.sync.dma_start(T.dx[:], T.x[:]).then_inc(S.ldx, 16)
+    g.scalar.wait_ge(S.ldx, 16)
+    g.scalar.dma_start(T.ws[:], T.w[:]).then_inc(S.ldw, 16)
+    g.sync.wait_ge(S.ldx, 16)
+    g.sync.dma_start(own, T.x[:]).then_inc(S.ldo, 16)
+
+    g.wait_ge(S.ldx, 16)
+    on = topo.mask(core, helpers[0])
+    off = topo.mask(core, jobs[core][0])
+    stay = _engines(on & ~off)
+    share = len(stay) // len(helpers)
+    trs = []
+    for i, h in enumerate(helpers):
+        rid, pid, _ = topo.addr(h)
+        trs.append(RemoteDMATransfer(dst_ids=[DstId(rid=rid, pnc=pid)],
+                                     dma_engine_mask=_join(stay[i * share:(i + 1) * share]),
+                                     remote_sem=S.relay, src=T.dx[:], dst=T.dx[:]))
+    g.remote_dma_fused(trs, local_sem=S.sent)
+    n = share * len(helpers) + _send(g, T, topo, core, rank, jobs[core])
+
+    if min(sign) < 0:
+        g.vector.memset(T.m1[:], -1.0).then_inc(S.fill, 1)
+        g.vector.wait_ge(S.fill, 1)
+        g.vector.wait_ge(S.ldw, 16)
+        g.vector.tensor_tensor(T.nw[:], T.ws[:], T.m1[:], AluOpType.mult).then_inc(S.neg, 1)
+
+    due = []
+    for j, (hs, jb) in enumerate(plan):
+        if j == rank:
+            due.append((0.0, j, 0))
+            continue
+        for s, ds in jb.items():
+            if core in ds:
+                late = 0.0 if s == cores[j] else 2.5
+                due.append((late + 1 + ds.index(core), j, len(_engines(topo.mask(s, core)))))
+    due.sort()
+
+    g.tensor.wait_ge(S.ldw, 16)
+    negated = False
+    for i, (_, j, inc) in enumerate(due):
+        if j == rank:
+            g.tensor.wait_ge(S.ldo, 16)
+        else:
+            g.tensor.wait_ge(S["a%d" % j], inc)
+        if sign[j] < 0 and not negated:
+            g.tensor.wait_ge(S.neg, 1)
+            negated = True
+        mm = g.tensor.matmul(T.acc[:], (T.ws if sign[j] > 0 else T.nw)[:], T.xin[:, j * C:(j + 1) * C],
+                             i == 0, i == len(due) - 1)
+    mm.then_inc(S.mm, 1)
+
+    g.vector.wait_ge(S.mm, 1)
+    g.vector.tensor_copy(T.ys[:], T.acc[:]).then_inc(S.cp, 1)
+    g.sync.wait_ge(S.cp, 1)
+    g.sync.dma_start(T.y[:], T.ys[:]).then_inc(S.st, 16)
+    g.sync.wait_ge(S.st, 16)
+    g.wait_ge(S.sent, n)

@@ -3,6 +3,7 @@ from concourse.mybir import AluOpType
 
 N = 8
 C = 512
+H = C // 2
 K = 128
 
 SCRATCH = {
@@ -12,24 +13,15 @@ SCRATCH = {
     "m1": ("sbuf", [128, K], "bfloat16"),
     "nw": ("sbuf", [128, K], "bfloat16"),
     "ys": ("sbuf", [128, C], "bfloat16"),
-    "acc": ("psum", [128, C], "float32"),
+    "acc0": ("psum", [128, C], "float32"),
+    "acc1": ("psum", [128, C], "float32"),
 }
-SEMAPHORES = ["ldx", "ldo", "ldw", "fill", "neg", "mm", "cp", "st", "relay", "sent"] + ["a%d" % j for j in range(N)]
-
-HELPERS = 2
-CAP_HELPER = 2
-CAP_RANK = 3
+SEMAPHORES = (["ldx", "ldo", "ldw", "fill", "neg", "mm0", "mm1", "cp0", "cp1", "st0", "st1", "relay", "sent"]
+              + ["a%d" % j for j in range(N)])
 
 
 def _engines(mask):
     return [1 << b for b in range(mask.bit_length()) if (mask >> b) & 1]
-
-
-def _join(bits):
-    m = 0
-    for b in bits:
-        m |= b
-    return m
 
 
 def _plan(T, topo):
@@ -43,21 +35,20 @@ def _plan(T, topo):
             return (cores.index(d) - j) % half
 
         plane = sorted([d for d in cores if topo.same_plane(ch, topo.chip(d))], key=rot)
-        cross = sorted([d for d in cores if d != me and d not in plane], key=rot)
-        cand = [c for c in range(topo.CHIPS * topo.CORES_PER_CHIP)
-                if topo.chip(c) == ch and c not in cores and topo.die(c) == topo.die(me)]
-        cand.sort(key=lambda c: not all(topo.may_write(c, d) for d in cross))
-        helpers = cand[:HELPERS]
-        senders = helpers + [me]
-        caps = [CAP_HELPER] * len(helpers) + [CAP_RANK]
-        jobs = {s: [] for s in senders}
-        for d in cross + plane:
-            for s, cap in zip(senders, caps):
-                if len(jobs[s]) < cap and topo.may_write(s, d):
-                    jobs[s].append(d)
-                    break
-        out.append((helpers, jobs))
+        cross = sorted([d for d in cores if d != me and d not in plane],
+                       key=lambda d: (not topo.mates(ch, topo.chip(d)), rot(d)))
+        own = [c for c in range(topo.CHIPS * topo.CORES_PER_CHIP) if topo.chip(c) == ch and c not in cores
+               and all(topo.may_write(c, d) for d in cross)]
+        a = [c for c in own if topo.die(c) != topo.die(me)][0]
+        b = [c for c in own if topo.die(c) == topo.die(me)][0]
+        out.append(([a, b], {a: cross[0:2], b: cross[2:], me: plane}))
     return out
+
+
+def _hand_masks(topo, me, helpers, far):
+    eng = _engines(topo.mask(me, helpers[0]) & ~topo.mask(me, far))
+    h = len(eng) // 2
+    return [sum(eng[:h]), sum(eng[h:])]
 
 
 def _send(g, T, topo, core, j, dests):
@@ -80,37 +71,28 @@ def rank_program(g, core, T, topo):
     if rank is None:
         for j, (helpers, jobs) in enumerate(plan):
             if core in helpers:
-                on = topo.mask(cores[j], core)
-                off = topo.mask(cores[j], jobs[cores[j]][0])
-                share = len(_engines(on & ~off)) // len(helpers)
-                g.wait_ge(S.relay, share)
+                masks = _hand_masks(topo, cores[j], helpers, jobs[cores[j]][0])
+                g.wait_ge(S.relay, len(_engines(masks[helpers.index(core)])))
                 n = _send(g, T, topo, core, j, jobs[core])
                 g.wait_ge(S.sent, n)
         return
 
     helpers, jobs = plan[rank]
     sign = T.tables["SIGN"][rank]
-    own = T.xin[:, rank * C:(rank + 1) * C]
 
     g.sync.dma_start(T.dx[:], T.x[:]).then_inc(S.ldx, 16)
     g.scalar.wait_ge(S.ldx, 16)
     g.scalar.dma_start(T.ws[:], T.w[:]).then_inc(S.ldw, 16)
     g.sync.wait_ge(S.ldx, 16)
-    g.sync.dma_start(own, T.x[:]).then_inc(S.ldo, 16)
+    g.sync.dma_start(T.xin[:, rank * C:(rank + 1) * C], T.x[:]).then_inc(S.ldo, 16)
 
     g.wait_ge(S.ldx, 16)
-    on = topo.mask(core, helpers[0])
-    off = topo.mask(core, jobs[core][0])
-    stay = _engines(on & ~off)
-    share = len(stay) // len(helpers)
-    trs = []
-    for i, h in enumerate(helpers):
-        rid, pid, _ = topo.addr(h)
-        trs.append(RemoteDMATransfer(dst_ids=[DstId(rid=rid, pnc=pid)],
-                                     dma_engine_mask=_join(stay[i * share:(i + 1) * share]),
-                                     remote_sem=S.relay, src=T.dx[:], dst=T.dx[:]))
-    g.remote_dma_fused(trs, local_sem=S.sent)
-    n = share * len(helpers) + _send(g, T, topo, core, rank, jobs[core])
+    masks = _hand_masks(topo, core, helpers, jobs[core][0])
+    where = [topo.addr(h) for h in helpers]
+    g.remote_dma_fused([RemoteDMATransfer(dst_ids=[DstId(rid=where[i][0], pnc=where[i][1])], dma_engine_mask=masks[i],
+                                          remote_sem=S.relay, src=T.dx[:], dst=T.dx[:]) for i in range(2)],
+                       local_sem=S.sent)
+    n = sum(len(_engines(m)) for m in masks) + _send(g, T, topo, core, rank, jobs[core])
 
     if min(sign) < 0:
         g.vector.memset(T.m1[:], -1.0).then_inc(S.fill, 1)
@@ -118,34 +100,43 @@ def rank_program(g, core, T, topo):
         g.vector.wait_ge(S.ldw, 16)
         g.vector.tensor_tensor(T.nw[:], T.ws[:], T.m1[:], AluOpType.mult).then_inc(S.neg, 1)
 
-    due = []
+    early, late = [(0, rank, 0)], []
     for j, (hs, jb) in enumerate(plan):
-        if j == rank:
-            due.append((0.0, j, 0))
-            continue
         for s, ds in jb.items():
             if core in ds:
-                late = 0.0 if s == cores[j] else 2.5
-                due.append((late + 1 + ds.index(core), j, len(_engines(topo.mask(s, core)))))
-    due.sort()
+                (early if s == cores[j] else late).append((ds.index(core), j, len(_engines(topo.mask(s, core)))))
+    early.sort()
+    late.sort()
+    ops = []
+    for _, j, inc in early:
+        ops += [(j, inc, 0), (j, inc, 1)]
+    for p in range(0, len(late), 2):
+        for hf in range(2):
+            ops += [(j, inc, hf) for _, j, inc in late[p:p + 2]]
 
+    acc = [T.acc0, T.acc1]
+    seen = []
     g.tensor.wait_ge(S.ldw, 16)
-    negated = False
-    for i, (_, j, inc) in enumerate(due):
-        if j == rank:
-            g.tensor.wait_ge(S.ldo, 16)
-        else:
-            g.tensor.wait_ge(S["a%d" % j], inc)
-        if sign[j] < 0 and not negated:
-            g.tensor.wait_ge(S.neg, 1)
-            negated = True
-        mm = g.tensor.matmul(T.acc[:], (T.ws if sign[j] > 0 else T.nw)[:], T.xin[:, j * C:(j + 1) * C],
-                             i == 0, i == len(due) - 1)
-    mm.then_inc(S.mm, 1)
+    for i, (j, inc, hf) in enumerate(ops):
+        if j not in seen:
+            if j == rank:
+                g.tensor.wait_ge(S.ldo, 16)
+            else:
+                g.tensor.wait_ge(S["a%d" % j], inc)
+            if sign[j] < 0 and min([1] + [sign[k] for k in seen]) > 0:
+                g.tensor.wait_ge(S.neg, 1)
+            seen.append(j)
+        first = hf not in [o[2] for o in ops[:i]]
+        last = hf not in [o[2] for o in ops[i + 1:]]
+        mm = g.tensor.matmul(acc[hf][:, 0:H], (T.ws if sign[j] > 0 else T.nw)[:],
+                             T.xin[:, j * C + hf * H:j * C + (hf + 1) * H], first, last)
+        if last:
+            mm.then_inc(S["mm%d" % hf], 1)
 
-    g.vector.wait_ge(S.mm, 1)
-    g.vector.tensor_copy(T.ys[:], T.acc[:]).then_inc(S.cp, 1)
-    g.sync.wait_ge(S.cp, 1)
-    g.sync.dma_start(T.y[:], T.ys[:]).then_inc(S.st, 16)
-    g.sync.wait_ge(S.st, 16)
+    for hf, q in ((0, g.scalar), (1, g.sync)):
+        g.vector.wait_ge(S["mm%d" % hf], 1)
+        g.vector.tensor_copy(T.ys[:, hf * H:(hf + 1) * H], acc[hf][:, 0:H]).then_inc(S["cp%d" % hf], 1)
+        q.wait_ge(S["cp%d" % hf], 1)
+        q.dma_start(T.y[:, hf * H:(hf + 1) * H], T.ys[:, hf * H:(hf + 1) * H]).then_inc(S["st%d" % hf], 16)
+        q.wait_ge(S["st%d" % hf], 16)
     g.wait_ge(S.sent, n)

from concourse.bass import DstId, RemoteDMATransfer
from concourse.mybir import AluOpType

N = 8
C = 512
H = C // 2
K = 128

SCRATCH = {
    "dx": ("dram", [128, C], "bfloat16"),
    "xin": ("sbuf", [128, N * C], "bfloat16"),
    "ws": ("sbuf", [128, K], "bfloat16"),
    "m1": ("sbuf", [128, K], "bfloat16"),
    "nw": ("sbuf", [128, K], "bfloat16"),
    "ys": ("sbuf", [128, C], "bfloat16"),
    "acc0": ("psum", [128, C], "float32"),
    "acc1": ("psum", [128, C], "float32"),
}
SEMAPHORES = (["ldx", "ldo", "ldw", "fill", "neg", "mm0", "mm1", "cp0", "cp1", "st0", "st1", "relay", "sent"]
              + ["a%d" % j for j in range(N)])


def _engines(mask):
    return [1 << b for b in range(mask.bit_length()) if (mask >> b) & 1]


def _plan(T, topo):
    cores = list(T.cores)
    half = len(cores) // 2
    out = []
    for j, me in enumerate(cores):
        ch = topo.chip(me)

        def rot(d):
            return (cores.index(d) - j) % half

        plane = sorted([d for d in cores if topo.same_plane(ch, topo.chip(d))], key=rot)
        cross = sorted([d for d in cores if d != me and d not in plane],
                       key=lambda d: (not topo.mates(ch, topo.chip(d)), rot(d)))
        own = [c for c in range(topo.CHIPS * topo.CORES_PER_CHIP) if topo.chip(c) == ch and c not in cores
               and all(topo.may_write(c, d) for d in cross)]
        a = [c for c in own if topo.die(c) != topo.die(me)][0]
        b = [c for c in own if topo.die(c) == topo.die(me)][0]
        out.append(([a, b], {a: cross[0:2], b: cross[2:], me: plane}))
    return out


def _hand_masks(topo, me, helpers, far):
    eng = _engines(topo.mask(me, helpers[0]) & ~topo.mask(me, far))
    h = len(eng) // 2
    return [sum(eng[:h]), sum(eng[h:])]


def _send(g, T, topo, core, j, dests):
    n = 0
    for d in dests:
        rid, pid, _ = topo.addr(d)
        m = topo.mask(core, d)
        g.remote_dma(out_ap=T.xin[:, j * C:(j + 1) * C], in_ap=T.dx[:], remote_sem=T.sem["a%d" % j],
                     local_sem=T.sem.sent, pid=pid, routing_id=rid, dma_engine_mask=m)
        n += len(_engines(m))
    return n


def rank_program(g, core, T, topo):
    S = T.sem
    plan = _plan(T, topo)
    cores = list(T.cores)
    rank = T.rank_of(core)

    if rank is None:
        for j, (helpers, jobs) in enumerate(plan):
            if core in helpers:
                masks = _hand_masks(topo, cores[j], helpers, jobs[cores[j]][0])
                g.wait_ge(S.relay, len(_engines(masks[helpers.index(core)])))
                n = _send(g, T, topo, core, j, jobs[core])
                g.wait_ge(S.sent, n)
        return

    helpers, jobs = plan[rank]
    sign = T.tables["SIGN"][rank]

    g.sync.dma_start(T.dx[:], T.x[:]).then_inc(S.ldx, 16)
    g.scalar.wait_ge(S.ldx, 16)
    g.scalar.dma_start(T.ws[:], T.w[:]).then_inc(S.ldw, 16)
    g.sync.wait_ge(S.ldx, 16)
    g.sync.dma_start(T.xin[:, rank * C:(rank + 1) * C], T.x[:]).then_inc(S.ldo, 16)

    g.wait_ge(S.ldx, 16)
    masks = _hand_masks(topo, core, helpers, jobs[core][0])
    where = [topo.addr(h) for h in helpers]
    g.remote_dma_fused([RemoteDMATransfer(dst_ids=[DstId(rid=where[i][0], pnc=where[i][1])], dma_engine_mask=masks[i],
                                          remote_sem=S.relay, src=T.dx[:], dst=T.dx[:]) for i in range(2)],
                       local_sem=S.sent)
    n = sum(len(_engines(m)) for m in masks) + _send(g, T, topo, core, rank, jobs[core])

    if min(sign) < 0:
        g.vector.memset(T.m1[:], -1.0).then_inc(S.fill, 1)
        g.vector.wait_ge(S.fill, 1)
        g.vector.wait_ge(S.ldw, 16)
        g.vector.tensor_tensor(T.nw[:], T.ws[:], T.m1[:], AluOpType.mult).then_inc(S.neg, 1)

    early, late = [(0, rank, 0)], []
    for j, (hs, jb) in enumerate(plan):
        for s, ds in jb.items():
            if core in ds:
                (early if s == cores[j] else late).append((ds.index(core), j, len(_engines(topo.mask(s, core)))))
    early.sort()
    late.sort()
    ops = []
    for _, j, inc in early:
        ops += [(j, inc, 0), (j, inc, 1)]
    for p in range(0, len(late), 2):
        for hf in range(2):
            ops += [(j, inc, hf) for _, j, inc in late[p:p + 2]]

    acc = [T.acc0, T.acc1]
    seen = []
    g.tensor.wait_ge(S.ldw, 16)
    for i, (j, inc, hf) in enumerate(ops):
        if j not in seen:
            if j == rank:
                g.tensor.wait_ge(S.ldo, 16)
            else:
                g.tensor.wait_ge(S["a%d" % j], inc)
            if sign[j] < 0 and min([1] + [sign[k] for k in seen]) > 0:
                g.tensor.wait_ge(S.neg, 1)
            seen.append(j)
        first = hf not in [o[2] for o in ops[:i]]
        last = hf not in [o[2] for o in ops[i + 1:]]
        mm = g.tensor.matmul(acc[hf][:, 0:H], (T.ws if sign[j] > 0 else T.nw)[:],
                             T.xin[:, j * C + hf * H:j * C + (hf + 1) * H], first, last)
        if last:
            mm.then_inc(S["mm%d" % hf], 1)

    for hf, q in ((0, g.scalar), (1, g.sync)):
        g.vector.wait_ge(S["mm%d" % hf], 1)
        g.vector.tensor_copy(T.ys[:, hf * H:(hf + 1) * H], acc[hf][:, 0:H]).then_inc(S["cp%d" % hf], 1)
        q.wait_ge(S["cp%d" % hf], 1)
        q.dma_start(T.y[:, hf * H:(hf + 1) * H], T.ys[:, hf * H:(hf + 1) * H]).then_inc(S["st%d" % hf], 16)
        q.wait_ge(S["st%d" % hf], 16)
    g.wait_ge(S.sent, n)
